import numpy as np
import ml_dtypes


def mxq(x, axis, fmt="e4m3"):
    dtype, down = {"e4m3": (ml_dtypes.float8_e4m3fn, 7), "e5m2": (ml_dtypes.float8_e5m2, 14)}[fmt]
    v = np.moveaxis(np.asarray(x, np.float32).astype(ml_dtypes.bfloat16).astype(np.float64), axis, -1)
    blocks = v.reshape(v.shape[:-1] + (-1, 32))
    amax = np.abs(blocks).max(-1, keepdims=True)
    byte = np.maximum(np.where(amax > 0, np.frexp(amax)[1] - 1 + 127, 0) - down, 1)
    scale = np.exp2(byte - 127.0)
    codes = (blocks / scale).astype(np.float32).astype(dtype).astype(np.float64)
    return np.moveaxis((codes * scale).reshape(v.shape), -1, axis)


WIDE = False


def mx_kscale(k):
    if not WIDE:
        return np.ones(k)
    levels = np.array([10, -10, 5, -5, 0])
    if k % 512:
        return np.exp2(np.random.permutation(np.resize(levels, k // 32))).repeat(32)
    a = np.empty((k // 512, 16))
    for p in range(k // 512):
        a[p, :8] = np.random.permutation(np.resize(levels, 8))
        for g in range(8):
            far = levels[np.abs(levels - a[p, g]) >= 10]
            a[p, g + 8] = far[np.random.randint(len(far))]
    return np.exp2(a.ravel()).repeat(32)


def f64(x):
    return np.asarray(x).astype(np.float64)


def striped(idx):
    return np.tile(idx.reshape(-1, 16).T, (8, 1)).astype(np.uint16)


def unstriped(offs):
    return offs[:16].T.reshape(-1).astype(np.int64)


E2M1 = np.array([0.0, 0.5, 1.0, 1.5, 2.0, 3.0, 4.0, 6.0, -0.0, -0.5, -1.0, -1.5, -2.0, -3.0, -4.0, -6.0])


def pack_weight(w, fmt):
    k, n = w.shape
    w = f64(np.asarray(w, np.float32).astype(ml_dtypes.bfloat16)).reshape(k // 32, 32, n)
    amax = np.abs(w).max(1)
    if fmt == "e4m3":
        byte = np.frexp(amax)[1] - 1 + 127 - 7
    else:
        mant, ex = np.frexp(amax / 6.0)
        byte = np.where(mant > 0.5, ex, ex - 1) + 127
    byte = np.clip(np.where(amax > 0, byte, 1), 1, 254)
    scaled = (w * np.exp2(127.0 - byte)[:, None, :]).reshape(k, n).astype(np.float32)
    by_word = np.ascontiguousarray(scaled.reshape(k // 512, 128, 4, n).transpose(0, 1, 3, 2))
    if fmt == "e4m3":
        words = by_word.astype(ml_dtypes.float8_e4m3fn).view(np.uint8)
    else:
        c = by_word.astype(ml_dtypes.float4_e2m1fn).view(np.uint8) & 0xF
        words = (c[..., 0::2] | (c[..., 1::2] << 4)).reshape(k // 512, 128, 2 * n)
    return np.ascontiguousarray(words), np.ascontiguousarray(byte.astype(np.uint8).reshape(k // 512, 16, n))


def unpack_weight(words, scales, fmt):
    g, _, n = scales.shape
    words = np.ascontiguousarray(words).reshape(g, 128, n, -1)
    if fmt == "e4m3":
        vals = words.view(ml_dtypes.float8_e4m3fn).astype(np.float64)
    else:
        nib = np.empty((g, 128, n, 4), np.uint8)
        nib[..., 0::2] = words & 0xF
        nib[..., 1::2] = words >> 4
        vals = E2M1[nib]
    vals = vals * np.repeat(np.exp2(scales.astype(np.float64) - 127.0), 8, axis=1)[..., None]
    return vals.transpose(0, 1, 3, 2).reshape(g * 512, n)


def gelu(v):
    return 0.5 * v * (1.0 + np.tanh(np.sqrt(2.0 / np.pi) * (v + 0.044715 * v**3)))


K, T, S, K2, TL, P, H, N = 1024, 4096, 1024, 512, 2048, 512, 1024, 512

def setup_inputs():
    n = np.random.standard_normal
    s = mx_kscale(K)[:, None]
    s2 = mx_kscale(K2)[:, None]
    u = mx_kscale(H)[:, None]
    d = {}
    d["tab_words"], d["tab_scales"] = pack_weight(n((K, T)) * s, "e4m3")
    d["tab2_words"], d["tab2_scales"] = pack_weight(n((K2, TL)) * s2, "e4m3")
    d["offs"] = striped(np.random.permutation(T)[:S])
    d["offs2"] = striped(np.random.permutation(TL)[:P])
    d["pos1"] = striped(np.random.permutation(S)[:P])
    d["w1_words"], d["w1_scales"] = pack_weight(1.5 * n((K, H)) / K**0.5 / s, "e2m1")
    d["w2"] = (0.8 * n((K2, H)) / K2**0.5 / s2).astype(np.float32)
    d["w3_words"], d["w3_scales"] = pack_weight(0.8 * n((K2, H)) / K2**0.5 / s2, "e4m3")
    d["wgs"] = np.exp(0.3 * n((128, P))).astype(np.float32)
    d["gain"] = (np.exp(0.3 * n(H)) * u[:, 0]).astype(np.float32)
    d["base"] = (0.7 * n((H, S)) * u).astype(np.float32)
    d["w4"] = (0.9 * n((H, N)) / H**0.5 / u).astype(np.float32)
    return d

def reference(tab_words, tab_scales, tab2_words, tab2_scales, offs, offs2, pos1, w1_words, w1_scales, w2, w3_words, w3_scales, wgs, gain, base, w4):
    v = unpack_weight(tab_words, tab_scales, "e4m3")[:, unstriped(offs)]
    v2 = unpack_weight(tab2_words, tab2_scales, "e4m3")[:, unstriped(offs2)]
    x = unpack_weight(w1_words, w1_scales, "e2m1").T @ v
    a = 0.5 * x * (1 + np.tanh(0.7978845608 * (x + 0.044715 * x**3)))
    sq = np.square(mxq(f64(w2), 0, "e4m3").T @ v2)
    b = sq + (unpack_weight(w3_words, w3_scales, "e4m3").T @ v2)
    placed = np.zeros((H, S))
    placed[:, unstriped(pos1)] = np.tile(f64(wgs), (H // 128, 1)) * b
    z = np.maximum(a, placed) * f64(gain)[:, None] + f64(base)
    return np.tanh(mxq(f64(w4), 0, "e4m3").T @ mxq(z, 0, "e4m3"))

@@ -1,0 +1,302 @@
+from contextlib import ExitStack
+
+import concourse.mybir as mybir
+from concourse.masks import make_identity
+
+K, T, S, K2, TL, NP, H, N = 1024, 4096, 1024, 512, 2048, 512, 1024, 512
+FLOPS = 2 * (K * H * S + 2 * K2 * H * NP + H * N * S)
+
+F32 = mybir.dt.float32
+BF16 = mybir.dt.bfloat16
+I32 = mybir.dt.int32
+U32 = mybir.dt.uint32
+U16 = mybir.dt.uint16
+U8 = mybir.dt.uint8
+FP8X4 = mybir.dt.float8_e4m3fn_x4
+FP4X4 = mybir.dt.float4_e2m1fn_x4
+ALU = mybir.AluOpType
+ACT = mybir.ActivationFunctionType
+
+P = 128
+BANK = 512
+ROW_TILES = H // P
+PAGES = 1
+GAIN_ON_VECTOR = ((7,0),(7,512))
+TAIL_ON_VECTOR = (("t",7,1),("b",1,0,1),("b",1,1,1))
+
+
+def tile_list_hop_offflavour_windows_kernel(
+    tc, tab_words, tab_scales, tab2_words, tab2_scales, offs, offs2, pos1,
+    w1_words, w1_scales, w2, w3_words, w3_scales, wgs, gain, base, w4, out,
+):
+    nc = tc.nc
+    with ExitStack() as ctx:
+        lists = ctx.enter_context(tc.tile_pool(name="lists", bufs=1))
+        keep = ctx.enter_context(tc.tile_pool(name="keep", bufs=1))
+        ring = ctx.enter_context(tc.tile_pool(name="ring", bufs=2))
+        psum = ctx.enter_context(tc.psum_pool(name="psum", bufs=1))
+
+        def held(name, shape, dtype):
+            return keep.tile(shape, dtype, name=name, align_bytes=64)
+
+        def bank(tag, shape):
+            return psum.tile(shape, F32, name=tag, tag=tag)
+
+        idx = lists.tile([P, S // 16], U16, name="idx")
+        idx2 = lists.tile([P, NP // 16], U16, name="idx2")
+        place = lists.tile([P, NP // 16], U16, name="place")
+
+        tab2_s = held("tab2_s", [P, TL], U8)
+        tab_s = held("tab_s", [P, T], U8)
+        w3_s = held("w3_s", [P, H], U8)
+        w1_s = held("w1_s", [P, 2, H], U8)
+        v_s1 = held("v_s1", [P, S], U8)
+        gain_rows = held("gain_rows", [P, P], F32)
+        pages = [held("page%d" % i, [P, S], F32) for i in range(PAGES)]
+        for plane in (tab2_s, w3_s):
+            nc.gpsimd.memset(plane[:].bitcast(I32), 0)
+        for plane in (tab_s, w1_s, v_s1):
+            nc.vector.memset(plane[:].bitcast(I32), 0)
+        nc.vector.memset(gain_rows[:], 0.0)
+        for page in pages:
+            nc.vector.memset(page[:], 0.0)
+
+        ident = held("ident", [P, P], F32)
+        make_identity(nc, ident[:])
+        tab2_w = held("tab2_w", [P, TL], I32)
+
+        w2_cut = (0, 128, 384, 640, 896, 1024)
+        w2_raw = [held("w2_raw%d" % i, [P, 4, w2_cut[i + 1] - w2_cut[i]], F32) for i in range(5)]
+        w4_raw = [held("w4_raw%d" % i, [P, 4, N], F32) for i in range(2)]
+        base_t = [held("base%d" % c, [P, S], F32) for c in range(ROW_TILES)]
+        tab_w = [held("tab_w%d" % a, [P, T], I32) for a in range(2)]
+        w3_first = held("w3_first", [P, P], I32)
+        w3_rest = held("w3_rest", [P, H - P], I32)
+        w3_view = w3_words[0].rearrange("p c i -> p (c i)").bitcast(I32)
+        w1_w = held("w1_w", [P, 2, 2 * H], U8)
+        wgs_t = held("wgs_t", [P, NP], F32)
+
+        def load_w2(i):
+            nc.sync.dma_start(w2_raw[i][:], w2[:, w2_cut[i] : w2_cut[i + 1]].rearrange("(p i) r -> p i r", i=4))
+
+        def load_base(c):
+            nc.sync.dma_start(base_t[c][:], base[P * c : P * (c + 1), :])
+
+        def load_tab(a):
+            nc.sync.dma_start(tab_w[a][:], tab_words[a].rearrange("p t i -> p (t i)").bitcast(I32))
+
+        def load_w4(b):
+            nc.sync.dma_start(w4_raw[b][:], w4[512 * b : 512 * (b + 1), :].rearrange("(p i) n -> p i n", i=4))
+
+        v2_s = held("v2_s", [P, NP], U8)
+        v2_w = held("v2_w", [P, NP], U32)
+        v_s0 = held("v_s0", [P, S], U8)
+
+        nc.sync.dma_start(idx[:], offs)
+        for q in range(4):
+            nc.sync.dma_start(tab_s[32 * q : 32 * q + 8, :].bitcast(I32), tab_scales[:, 4 * q : 4 * q + 4, :].bitcast(I32))
+        load_w2(0)
+        nc.sync.dma_start(tab2_w[:], tab2_words[0].rearrange("p t i -> p (t i)").bitcast(I32))
+        nc.sync.dma_start(idx2[:], offs2)
+        for q in range(4):
+            nc.sync.dma_start(tab2_s[32 * q : 32 * q + 4, :].bitcast(I32), tab2_scales[0, 4 * q : 4 * q + 4, :].bitcast(I32))
+        for q in range(4):
+            nc.sync.dma_start(w3_s[32 * q : 32 * q + 4, :].bitcast(I32), w3_scales[0, 4 * q : 4 * q + 4, :].bitcast(I32))
+        nc.sync.dma_start(w3_first[:], w3_view[:, 0:P])
+        nc.sync.dma_start(wgs_t[:], wgs)
+        nc.sync.dma_start(place[:], pos1)
+        load_tab(0)
+        nc.vector.tensor_copy(v_s0[:], tab_s[:].indirect(idx[:]))
+        nc.vector.tensor_copy(v2_w[:], tab2_w[:].bitcast(U32).indirect(idx2[:]))
+        nc.vector.tensor_copy(v2_s[:], tab2_s[:].indirect(idx2[:]))
+        for q in range(4):
+            nc.sync.dma_start(v_s1[32 * q : 32 * q + 4, :].bitcast(I32), v_s0[32 * q + 4 : 32 * q + 8, :].bitcast(I32))
+        load_tab(1)
+        nc.sync.dma_start(w1_w[:].bitcast(I32), w1_words.rearrange("a p n -> p a n").bitcast(I32))
+        for q in range(4):
+            nc.sync.dma_start(
+                w1_s[32 * q : 32 * q + 4, :, :].bitcast(I32),
+                w1_scales[:, 4 * q : 4 * q + 4, :].rearrange("a r n -> r a n").bitcast(I32),
+            )
+        nc.gpsimd.dma_start(gain_rows[0:ROW_TILES, :], gain.rearrange("(c p) -> c p", p=P))
+        load_w2(1)
+        nc.sync.dma_start(w3_rest[:], w3_view[:, P:H])
+        load_w2(2)
+        load_base(0)
+        load_base(1)
+        load_w2(3)
+        load_base(2)
+        load_w2(4)
+        load_base(3)
+        load_w4(0)
+        load_base(4)
+        load_w4(1)
+        load_base(5)
+        load_base(6)
+        load_base(7)
+
+        v_s = (v_s0, v_s1)
+        v_w = [[held("v_w%d%d" % (a, h), [P, BANK], U32) for h in range(2)] for a in range(2)]
+
+        def gather_tab(a):
+            for h in range(2):
+                nc.vector.tensor_copy(v_w[a][h][:], tab_w[a][:].bitcast(U32).indirect(idx[:, 32 * h : 32 * (h + 1)]))
+
+        gain_col = held("gain_col", [P, ROW_TILES], F32)
+
+        def quantised(name, raw, width):
+            grouped = ring.tile([P, width, 4], BF16, name="grouped", tag="grouped", align_bytes=64)
+            nc.scalar.copy(
+                grouped[:].rearrange("p (c i) t -> p c t i", i=4),
+                raw[:].rearrange("p t (c i) -> p c t i", i=4),
+            )
+            codes = held(name + "_c", [P, width], U32)
+            scales = held(name + "_s", [P, width], U8)
+            nc.vector.quantize_mx(out=codes[:].bitcast(FP8X4), scales=scales[:], in_=grouped[:].rearrange("p w t -> p (w t)"))
+            return codes, scales
+
+        w2_q = {}
+        w4_q = {}
+        feat = {}
+        both = {}
+        z_t = {}
+        z_q = {}
+        acc = {}
+
+        def assay(c):
+            piece = max(i for i in range(5) if w2_cut[i] <= P * c)
+            codes, scales = w2_q[piece]
+            own = slice(P * c - w2_cut[piece], P * (c + 1) - w2_cut[piece])
+            cols = slice(P * c, P * (c + 1))
+            w3_cols = w3_first[:] if c == 0 else w3_rest[:, P * (c - 1) : P * c]
+            y2 = bank("y2", [P, BANK])
+            y3 = bank("y3", [P, BANK])
+            nc.tensor.matmul_mx(out=y2[:], lhsT=codes[:, own].bitcast(FP8X4), lhsT_scale=scales[:, own],
+                                rhs=v2_w[:].bitcast(FP8X4), rhs_scale=v2_s[:], start=True, stop=True)
+            nc.tensor.matmul_mx(out=y3[:], lhsT=w3_cols.bitcast(FP8X4), lhsT_scale=w3_s[:, cols],
+                                rhs=v2_w[:].bitcast(FP8X4), rhs_scale=v2_s[:], start=True, stop=True)
+            sq = ring.tile([P, NP], F32, name="sq")
+            nc.scalar.activation(sq[:], y2[:], ACT.Square)
+            both[c] = ring.tile([P, NP], F32, name="both")
+            nc.vector.tensor_tensor(both[c][:], y3[:], sq[:], ALU.add)
+
+        def put(c):
+            nc.vector.tensor_tensor(pages[min(c, PAGES - 1)][:].indirect(place[:]), both[c][:], wgs_t[:], ALU.mult)
+
+        def sensor(c):
+            feat[c] = ring.tile([P, S], F32, name="feat", bufs=3)
+            for h in range(2):
+                x = bank("x%d" % h, [P, BANK])
+                for a in range(2):
+                    nc.tensor.matmul_mx(
+                        out=x[:], lhsT=w1_w[:, a, 2 * P * c : 2 * P * (c + 1)].bitcast(FP4X4),
+                        lhsT_scale=w1_s[:, a, P * c : P * (c + 1)],
+                        rhs=v_w[a][h][:].bitcast(FP8X4), rhs_scale=v_s[a][:, BANK * h : BANK * (h + 1)],
+                        start=(a == 0), stop=(a == 1),
+                    )
+                nc.scalar.activation(feat[c][:, BANK * h : BANK * (h + 1)], x[:], ACT.Gelu_apprx_tanh)
+
+        def combine(c, halves):
+            b, cc = divmod(c, 4)
+            f = feat[c]
+            for cols in halves:
+                nc.vector.tensor_tensor(f[:, cols], f[:, cols], pages[min(c, PAGES - 1)][:, cols], ALU.max)
+                if (c, cols.start) in GAIN_ON_VECTOR:
+                    nc.vector.tensor_scalar(f[:, cols], f[:, cols], gain_col[:, c : c + 1], None, ALU.mult)
+                else:
+                    nc.scalar.activation(f[:, cols], f[:, cols], ACT.Copy, scale=gain_col[:, c : c + 1])
+            for h in range(2):
+                if cc == 0:
+                    z_t[b, h] = held("z_t%d%d" % (b, h), [P, 4, 2, P, 2], BF16)
+                turned = bank("turn%d" % h, [P, 4, P])
+                for step, src in enumerate((base_t[c], f)):
+                    for k in range(4):
+                        j0 = BANK * h + P * k
+                        nc.tensor.matmul(turned[:, k, :], src[:, j0 : j0 + P], ident[:], is_transpose=True,
+                                         start=(step == 0 and k == 0), stop=(step == 1 and k == 3))
+                copy = nc.vector.tensor_copy if ("t", c, h) in TAIL_ON_VECTOR else nc.scalar.copy
+                copy(
+                    z_t[b, h][:, :, :, 32 * cc : 32 * (cc + 1), :],
+                    turned[:].rearrange("j k (p u e) -> j k u p e", u=2, e=2),
+                )
+
+        def turn_back(b, h):
+            words = z_t[b, h][:].rearrange("j k u p e -> j (k u p e)").bitcast(F32)
+            grouped = ring.tile([P, BANK * 4], BF16, name="z_grouped", align_bytes=64)
+            pairs = grouped[:].bitcast(F32).rearrange("p (j u) -> p j u", u=2)
+            for quarter in range(2):
+                back = bank("back%d" % quarter, [P, 2, 2 * P])
+                for k in range(2):
+                    for u in range(2):
+                        w0 = P * (2 * (2 * quarter + k) + u)
+                        nc.tensor.transpose(back[:, u, P * k : P * (k + 1)], words[:, w0 : w0 + P], ident[:])
+                copy = nc.vector.tensor_copy if ("b", b, h, quarter) in TAIL_ON_VECTOR else nc.scalar.copy
+                copy(pairs[:, 256 * quarter : 256 * (quarter + 1), :], back[:].rearrange("p u j -> p j u"))
+            codes = held("z_c%d%d" % (b, h), [P, BANK], U32)
+            scales = held("z_s%d%d" % (b, h), [P, BANK], U8)
+            nc.vector.quantize_mx(out=codes[:].bitcast(FP8X4), scales=scales[:], in_=grouped[:])
+            z_q[b, h] = (codes, scales)
+
+        out_banks = (("y2", "y3", "x0", "x1"), ("turn0", "turn1", "back0", "back1"))
+
+        def last_product(b, h, tiles):
+            wc, ws = w4_q[b]
+            zc, zs = z_q[b, h]
+            for n in tiles:
+                if b == 0:
+                    acc[n, h] = bank(out_banks[h][n], [P, BANK])
+                cols = slice(P * n, P * (n + 1))
+                nc.tensor.matmul_mx(out=acc[n, h][:], lhsT=wc[:, cols].bitcast(FP8X4), lhsT_scale=ws[:, cols],
+                                    rhs=zc[:].bitcast(FP8X4), rhs_scale=zs[:], start=(b == 0), stop=(b == 1))
+                if b == 1:
+                    res = ring.tile([P, BANK], F32, name="res", bufs=8)
+                    nc.scalar.activation(res[:], acc[n, h][:], ACT.Tanh)
+                    nc.sync.dma_start(out[cols, BANK * h : BANK * (h + 1)], res[:])
+
+        whole = [slice(0, S)]
+        by_half = [slice(0, BANK), slice(BANK, S)]
+
+        def w2_piece(i):
+            w2_q[i] = quantised("w2q%d" % i, w2_raw[i], w2_cut[i + 1] - w2_cut[i])
+
+        w2_piece(0)
+        assay(0)
+        put(0)
+        gather_tab(0)
+        gather_tab(1)
+        gain_ps = bank("back0", [P, P])
+        nc.tensor.transpose(gain_ps[:], gain_rows[:], ident[:])
+        nc.scalar.copy(gain_col[:], gain_ps[:, 0:ROW_TILES])
+        sensor(0)
+        w2_piece(1)
+        assay(1)
+        pass
+        w2_piece(2)
+        for c in range(ROW_TILES):
+            if c in (1, 2):
+                w2_piece(3 + (1, 2).index(c))
+            if c + 1 < ROW_TILES:
+                sensor(c + 1)
+            if c + 2 < ROW_TILES:
+                assay(c + 2)
+            combine(c, by_half if c == ROW_TILES - 1 else whole)
+            if 0 < c + 1 < ROW_TILES:
+                put(c + 1)
+            if c == 2:
+                w4_q[0] = quantised("w4q0", w4_raw[0], N)
+            if c == 3:
+                w4_q[1] = quantised("w4q1", w4_raw[1], N)
+            if c == 4:
+                turn_back(0, 0)
+            if c == 4+0:
+                turn_back(0, 1)
+            if c == 6:
+                last_product(0, 0, range(4))
+        turn_back(1, 0)
+        last_product(0, 1, range(2))
+        last_product(1, 0, range(4))
+        turn_back(1, 1)
+        last_product(1, 1, range(2))
+        for n in (2, 3):
+            last_product(0, 1, [n])
+            last_product(1, 1, [n])

@@ -53,9 +53,9 @@ def tile_list_hop_offflavour_windows_kernel(
         v_s1 = held("v_s1", [P, S], U8)
         gain_rows = held("gain_rows", [P, P], F32)
         pages = [held("page%d" % i, [P, S], F32) for i in range(PAGES)]
-        for plane in (tab2_s, w3_s):
+        for plane in (tab_s,):
             nc.gpsimd.memset(plane[:].bitcast(I32), 0)
-        for plane in (tab_s, w1_s, v_s1):
+        for plane in (tab2_s, w3_s, w1_s, v_s1):
             nc.vector.memset(plane[:].bitcast(I32), 0)
         nc.vector.memset(gain_rows[:], 0.0)
         for page in pages:
@@ -65,13 +65,13 @@ def tile_list_hop_offflavour_windows_kernel(
         make_identity(nc, ident[:])
         tab2_w = held("tab2_w", [P, TL], I32)
 
-        w2_cut = (0, 128, 384, 640, 896, 1024)
+        w2_cut = (0, 128, 256, 512, 768, 1024)
         w2_raw = [held("w2_raw%d" % i, [P, 4, w2_cut[i + 1] - w2_cut[i]], F32) for i in range(5)]
         w4_raw = [held("w4_raw%d" % i, [P, 4, N], F32) for i in range(2)]
         base_t = [held("base%d" % c, [P, S], F32) for c in range(ROW_TILES)]
         tab_w = [held("tab_w%d" % a, [P, T], I32) for a in range(2)]
-        w3_first = held("w3_first", [P, P], I32)
-        w3_rest = held("w3_rest", [P, H - P], I32)
+        w3_first = held("w3_first", [P, 2 * P], I32)
+        w3_rest = held("w3_rest", [P, H - 2 * P], I32)
         w3_view = w3_words[0].rearrange("p c i -> p (c i)").bitcast(I32)
         w1_w = held("w1_w", [P, 2, 2 * H], U8)
         wgs_t = held("wgs_t", [P, NP], F32)
@@ -93,18 +93,19 @@ def tile_list_hop_offflavour_windows_kernel(
         v_s0 = held("v_s0", [P, S], U8)
 
         nc.sync.dma_start(idx[:], offs)
+        nc.sync.dma_start(idx2[:], offs2)
+        nc.sync.dma_start(place[:], pos1)
+        load_w2(0)
         for q in range(4):
             nc.sync.dma_start(tab_s[32 * q : 32 * q + 8, :].bitcast(I32), tab_scales[:, 4 * q : 4 * q + 4, :].bitcast(I32))
-        load_w2(0)
         nc.sync.dma_start(tab2_w[:], tab2_words[0].rearrange("p t i -> p (t i)").bitcast(I32))
-        nc.sync.dma_start(idx2[:], offs2)
         for q in range(4):
             nc.sync.dma_start(tab2_s[32 * q : 32 * q + 4, :].bitcast(I32), tab2_scales[0, 4 * q : 4 * q + 4, :].bitcast(I32))
+        nc.sync.dma_start(w3_first[:], w3_view[:, 0 : 2 * P])
+        nc.sync.dma_start(wgs_t[:], wgs)
         for q in range(4):
             nc.sync.dma_start(w3_s[32 * q : 32 * q + 4, :].bitcast(I32), w3_scales[0, 4 * q : 4 * q + 4, :].bitcast(I32))
-        nc.sync.dma_start(w3_first[:], w3_view[:, 0:P])
-        nc.sync.dma_start(wgs_t[:], wgs)
-        nc.sync.dma_start(place[:], pos1)
+        load_w2(1)
         load_tab(0)
         nc.vector.tensor_copy(v_s0[:], tab_s[:].indirect(idx[:]))
         nc.vector.tensor_copy(v2_w[:], tab2_w[:].bitcast(U32).indirect(idx2[:]))
@@ -119,28 +120,31 @@ def tile_list_hop_offflavour_windows_kernel(
                 w1_scales[:, 4 * q : 4 * q + 4, :].rearrange("a r n -> r a n").bitcast(I32),
             )
         nc.gpsimd.dma_start(gain_rows[0:ROW_TILES, :], gain.rearrange("(c p) -> c p", p=P))
-        load_w2(1)
-        nc.sync.dma_start(w3_rest[:], w3_view[:, P:H])
         load_w2(2)
+        nc.sync.dma_start(w3_rest[:], w3_view[:, 2 * P : H])
         load_base(0)
-        load_base(1)
         load_w2(3)
-        load_base(2)
+        load_base(1)
         load_w2(4)
-        load_base(3)
+        load_base(2)
         load_w4(0)
-        load_base(4)
+        load_base(3)
         load_w4(1)
+        load_base(4)
         load_base(5)
         load_base(6)
         load_base(7)
 
         v_s = (v_s0, v_s1)
-        v_w = [[held("v_w%d%d" % (a, h), [P, BANK], U32) for h in range(2)] for a in range(2)]
+        v_w = [held("v_w%d" % a, [P, S], U32) for a in range(2)]
 
         def gather_tab(a):
-            for h in range(2):
-                nc.vector.tensor_copy(v_w[a][h][:], tab_w[a][:].bitcast(U32).indirect(idx[:, 32 * h : 32 * (h + 1)]))
+            window = tab_w[a][:].bitcast(U32)
+            if a == 0:
+                nc.vector.tensor_copy(v_w[0][:], window.indirect(idx[:]))
+            else:
+                for h in range(2):
+                    nc.vector.tensor_copy(v_w[1][:, BANK * h : BANK * (h + 1)], window.indirect(idx[:, 32 * h : 32 * (h + 1)]))
 
         gain_col = held("gain_col", [P, ROW_TILES], F32)
 
@@ -168,9 +172,9 @@ def tile_list_hop_offflavour_windows_kernel(
             codes, scales = w2_q[piece]
             own = slice(P * c - w2_cut[piece], P * (c + 1) - w2_cut[piece])
             cols = slice(P * c, P * (c + 1))
-            w3_cols = w3_first[:] if c == 0 else w3_rest[:, P * (c - 1) : P * c]
+            w3_cols = w3_first[:, P * c : P * (c + 1)] if c < 2 else w3_rest[:, P * (c - 2) : P * (c - 1)]
             y2 = bank("y2", [P, BANK])
-            y3 = bank("y3", [P, BANK])
+            y3 = bank(("y3", "back1")[c % 2], [P, BANK])
             nc.tensor.matmul_mx(out=y2[:], lhsT=codes[:, own].bitcast(FP8X4), lhsT_scale=scales[:, own],
                                 rhs=v2_w[:].bitcast(FP8X4), rhs_scale=v2_s[:], start=True, stop=True)
             nc.tensor.matmul_mx(out=y3[:], lhsT=w3_cols.bitcast(FP8X4), lhsT_scale=w3_s[:, cols],
@@ -191,7 +195,7 @@ def tile_list_hop_offflavour_windows_kernel(
                     nc.tensor.matmul_mx(
                         out=x[:], lhsT=w1_w[:, a, 2 * P * c : 2 * P * (c + 1)].bitcast(FP4X4),
                         lhsT_scale=w1_s[:, a, P * c : P * (c + 1)],
-                        rhs=v_w[a][h][:].bitcast(FP8X4), rhs_scale=v_s[a][:, BANK * h : BANK * (h + 1)],
+                        rhs=v_w[a][:, BANK * h : BANK * (h + 1)].bitcast(FP8X4), rhs_scale=v_s[a][:, BANK * h : BANK * (h + 1)],
                         start=(a == 0), stop=(a == 1),
                     )
                 nc.scalar.activation(feat[c][:, BANK * h : BANK * (h + 1)], x[:], ACT.Gelu_apprx_tanh)
@@ -225,7 +229,7 @@ def tile_list_hop_offflavour_windows_kernel(
             grouped = ring.tile([P, BANK * 4], BF16, name="z_grouped", align_bytes=64)
             pairs = grouped[:].bitcast(F32).rearrange("p (j u) -> p j u", u=2)
             for quarter in range(2):
-                back = bank("back%d" % quarter, [P, 2, 2 * P])
+                back = bank("back%d" % (quarter * b), [P, 2, 2 * P])
                 for k in range(2):
                     for u in range(2):
                         w0 = P * (2 * (2 * quarter + k) + u)
@@ -262,33 +266,33 @@ def tile_list_hop_offflavour_windows_kernel(
         w2_piece(0)
         assay(0)
         put(0)
+        w2_piece(1)
+        assay(1)
         gather_tab(0)
         gather_tab(1)
         gain_ps = bank("back0", [P, P])
         nc.tensor.transpose(gain_ps[:], gain_rows[:], ident[:])
         nc.scalar.copy(gain_col[:], gain_ps[:, 0:ROW_TILES])
         sensor(0)
-        w2_piece(1)
-        assay(1)
         pass
         w2_piece(2)
         for c in range(ROW_TILES):
-            if c in (1, 2):
-                w2_piece(3 + (1, 2).index(c))
-            if c + 1 < ROW_TILES:
-                sensor(c + 1)
+            if c in (0, 1):
+                w2_piece(3 + (0, 1).index(c))
             if c + 2 < ROW_TILES:
                 assay(c + 2)
+            if c + 1 < ROW_TILES:
+                sensor(c + 1)
             combine(c, by_half if c == ROW_TILES - 1 else whole)
             if 0 < c + 1 < ROW_TILES:
                 put(c + 1)
-            if c == 2:
+            if c == 1:
                 w4_q[0] = quantised("w4q0", w4_raw[0], N)
-            if c == 3:
+            if c == 2:
                 w4_q[1] = quantised("w4q1", w4_raw[1], N)
-            if c == 4:
+            if c == 3:
                 turn_back(0, 0)
-            if c == 4+0:
+            if c == 3+0:
                 turn_back(0, 1)
             if c == 6:
                 last_product(0, 0, range(4))

@@ -50,16 +50,11 @@ def tile_list_hop_offflavour_windows_kernel(
         tab_s = held("tab_s", [P, T], U8)
         w3_s = held("w3_s", [P, H], U8)
         w1_s = held("w1_s", [P, 2, H], U8)
-        v_s1 = held("v_s1", [P, S], U8)
+        v_s = held("v_s", [P, 2, S], U8)
         gain_rows = held("gain_rows", [P, P], F32)
         pages = [held("page%d" % i, [P, S], F32) for i in range(PAGES)]
-        for plane in (tab_s,):
-            nc.gpsimd.memset(plane[:].bitcast(I32), 0)
-        for plane in (tab2_s, w3_s, w1_s, v_s1):
-            nc.vector.memset(plane[:].bitcast(I32), 0)
-        nc.vector.memset(gain_rows[:], 0.0)
-        for page in pages:
-            nc.vector.memset(page[:], 0.0)
+        for plane in (tab2_s[:], w3_s[:], tab_s[0:96, :]):
+            nc.vector.memset(plane.bitcast(I32), 0)
 
         ident = held("ident", [P, P], F32)
         make_identity(nc, ident[:])
@@ -93,25 +88,30 @@ def tile_list_hop_offflavour_windows_kernel(
         v_s0 = held("v_s0", [P, S], U8)
 
         nc.sync.dma_start(idx[:], offs)
+        nc.sync.dma_start(tab_s[96:128, :].bitcast(I32), tab_scales.rearrange("a q t -> (a q) t").bitcast(I32))
         nc.sync.dma_start(idx2[:], offs2)
-        nc.sync.dma_start(place[:], pos1)
-        load_w2(0)
-        for q in range(4):
-            nc.sync.dma_start(tab_s[32 * q : 32 * q + 8, :].bitcast(I32), tab_scales[:, 4 * q : 4 * q + 4, :].bitcast(I32))
         nc.sync.dma_start(tab2_w[:], tab2_words[0].rearrange("p t i -> p (t i)").bitcast(I32))
         for q in range(4):
             nc.sync.dma_start(tab2_s[32 * q : 32 * q + 4, :].bitcast(I32), tab2_scales[0, 4 * q : 4 * q + 4, :].bitcast(I32))
+        load_w2(0)
         nc.sync.dma_start(w3_first[:], w3_view[:, 0 : 2 * P])
+        nc.sync.dma_start(place[:], pos1)
         nc.sync.dma_start(wgs_t[:], wgs)
         for q in range(4):
             nc.sync.dma_start(w3_s[32 * q : 32 * q + 4, :].bitcast(I32), w3_scales[0, 4 * q : 4 * q + 4, :].bitcast(I32))
         load_w2(1)
         load_tab(0)
-        nc.vector.tensor_copy(v_s0[:], tab_s[:].indirect(idx[:]))
-        nc.vector.tensor_copy(v2_w[:], tab2_w[:].bitcast(U32).indirect(idx2[:]))
         nc.vector.tensor_copy(v2_s[:], tab2_s[:].indirect(idx2[:]))
-        for q in range(4):
-            nc.sync.dma_start(v_s1[32 * q : 32 * q + 4, :].bitcast(I32), v_s0[32 * q + 4 : 32 * q + 8, :].bitcast(I32))
+        nc.vector.tensor_copy(v2_w[:], tab2_w[:].bitcast(U32).indirect(idx2[:]))
+        nc.vector.tensor_copy(v_s0[:], tab_s[:].indirect(idx[:]))
+        for plane in (v_s, w1_s):
+            nc.vector.memset(plane[:].bitcast(I32), 0)
+        nc.vector.memset(pages[0][:], 0.0)
+        nc.vector.memset(gain_rows[:], 0.0)
+        for a in range(2):
+            for q in range(4):
+                row = 96 + 16 * a + 4 * q
+                nc.gpsimd.dma_start(v_s[32 * q : 32 * q + 4, a, :].bitcast(I32), v_s0[row : row + 4, :].bitcast(I32))
         load_tab(1)
         nc.sync.dma_start(w1_w[:].bitcast(I32), w1_words.rearrange("a p n -> p a n").bitcast(I32))
         for q in range(4):
@@ -119,7 +119,7 @@ def tile_list_hop_offflavour_windows_kernel(
                 w1_s[32 * q : 32 * q + 4, :, :].bitcast(I32),
                 w1_scales[:, 4 * q : 4 * q + 4, :].rearrange("a r n -> r a n").bitcast(I32),
             )
-        nc.gpsimd.dma_start(gain_rows[0:ROW_TILES, :], gain.rearrange("(c p) -> c p", p=P))
+        nc.sync.dma_start(gain_rows[0:ROW_TILES, :], gain.rearrange("(c p) -> c p", p=P))
         load_w2(2)
         nc.sync.dma_start(w3_rest[:], w3_view[:, 2 * P : H])
         load_base(0)
@@ -135,7 +135,6 @@ def tile_list_hop_offflavour_windows_kernel(
         load_base(6)
         load_base(7)
 
-        v_s = (v_s0, v_s1)
         v_w = [held("v_w%d" % a, [P, S], U32) for a in range(2)]
 
         def gather_tab(a):
@@ -195,7 +194,7 @@ def tile_list_hop_offflavour_windows_kernel(
                     nc.tensor.matmul_mx(
                         out=x[:], lhsT=w1_w[:, a, 2 * P * c : 2 * P * (c + 1)].bitcast(FP4X4),
                         lhsT_scale=w1_s[:, a, P * c : P * (c + 1)],
-                        rhs=v_w[a][:, BANK * h : BANK * (h + 1)].bitcast(FP8X4), rhs_scale=v_s[a][:, BANK * h : BANK * (h + 1)],
+                        rhs=v_w[a][:, BANK * h : BANK * (h + 1)].bitcast(FP8X4), rhs_scale=v_s[:, a, BANK * h : BANK * (h + 1)],
                         start=(a == 0), stop=(a == 1),
                     )
                 nc.scalar.activation(feat[c][:, BANK * h : BANK * (h + 1)], x[:], ACT.Gelu_apprx_tanh)

from contextlib import ExitStack

import concourse.mybir as mybir
from concourse.masks import make_identity

K, T, S, K2, TL, NP, H, N = 1024, 4096, 1024, 512, 2048, 512, 1024, 512
FLOPS = 2 * (K * H * S + 2 * K2 * H * NP + H * N * S)

F32 = mybir.dt.float32
BF16 = mybir.dt.bfloat16
I32 = mybir.dt.int32
U32 = mybir.dt.uint32
U16 = mybir.dt.uint16
U8 = mybir.dt.uint8
FP8X4 = mybir.dt.float8_e4m3fn_x4
FP4X4 = mybir.dt.float4_e2m1fn_x4
ALU = mybir.AluOpType
ACT = mybir.ActivationFunctionType

P = 128
BANK = 512
ROW_TILES = H // P
PAGES = 1
GAIN_ON_VECTOR = ((7,0),(7,512))
TAIL_ON_VECTOR = (("t",7,1),("b",1,0,1),("b",1,1,1))


def tile_list_hop_offflavour_windows_kernel(
    tc, tab_words, tab_scales, tab2_words, tab2_scales, offs, offs2, pos1,
    w1_words, w1_scales, w2, w3_words, w3_scales, wgs, gain, base, w4, out,
):
    nc = tc.nc
    with ExitStack() as ctx:
        lists = ctx.enter_context(tc.tile_pool(name="lists", bufs=1))
        keep = ctx.enter_context(tc.tile_pool(name="keep", bufs=1))
        ring = ctx.enter_context(tc.tile_pool(name="ring", bufs=2))
        psum = ctx.enter_context(tc.psum_pool(name="psum", bufs=1))

        def held(name, shape, dtype):
            return keep.tile(shape, dtype, name=name, align_bytes=64)

        def bank(tag, shape):
            return psum.tile(shape, F32, name=tag, tag=tag)

        idx = lists.tile([P, S // 16], U16, name="idx")
        idx2 = lists.tile([P, NP // 16], U16, name="idx2")
        place = lists.tile([P, NP // 16], U16, name="place")

        tab2_s = held("tab2_s", [P, TL], U8)
        tab_s = held("tab_s", [P, T], U8)
        w3_s = held("w3_s", [P, H], U8)
        w1_s = held("w1_s", [P, 2, H], U8)
        v_s = held("v_s", [P, 2, S], U8)
        gain_rows = held("gain_rows", [P, P], F32)
        pages = [held("page%d" % i, [P, S], F32) for i in range(PAGES)]
        for plane in (tab2_s[:], w3_s[:], tab_s[0:96, :]):
            nc.vector.memset(plane.bitcast(I32), 0)

        ident = held("ident", [P, P], F32)
        make_identity(nc, ident[:])
        tab2_w = held("tab2_w", [P, TL], I32)

        w2_cut = (0, 128, 256, 512, 768, 1024)
        w2_raw = [held("w2_raw%d" % i, [P, 4, w2_cut[i + 1] - w2_cut[i]], F32) for i in range(5)]
        w4_raw = [held("w4_raw%d" % i, [P, 4, N], F32) for i in range(2)]
        base_t = [held("base%d" % c, [P, S], F32) for c in range(ROW_TILES)]
        tab_w = [held("tab_w%d" % a, [P, T], I32) for a in range(2)]
        w3_first = held("w3_first", [P, 2 * P], I32)
        w3_rest = held("w3_rest", [P, H - 2 * P], I32)
        w3_view = w3_words[0].rearrange("p c i -> p (c i)").bitcast(I32)
        w1_w = held("w1_w", [P, 2, 2 * H], U8)
        wgs_t = held("wgs_t", [P, NP], F32)

        def load_w2(i):
            nc.sync.dma_start(w2_raw[i][:], w2[:, w2_cut[i] : w2_cut[i + 1]].rearrange("(p i) r -> p i r", i=4))

        def load_base(c):
            nc.sync.dma_start(base_t[c][:], base[P * c : P * (c + 1), :])

        def load_tab(a):
            nc.sync.dma_start(tab_w[a][:], tab_words[a].rearrange("p t i -> p (t i)").bitcast(I32))

        def load_w4(b):
            nc.sync.dma_start(w4_raw[b][:], w4[512 * b : 512 * (b + 1), :].rearrange("(p i) n -> p i n", i=4))

        v2_s = held("v2_s", [P, NP], U8)
        v2_w = held("v2_w", [P, NP], U32)
        v_s0 = held("v_s0", [P, S], U8)

        nc.sync.dma_start(idx[:], offs)
        nc.sync.dma_start(tab_s[96:128, :].bitcast(I32), tab_scales.rearrange("a q t -> (a q) t").bitcast(I32))
        nc.sync.dma_start(idx2[:], offs2)
        nc.sync.dma_start(tab2_w[:], tab2_words[0].rearrange("p t i -> p (t i)").bitcast(I32))
        for q in range(4):
            nc.sync.dma_start(tab2_s[32 * q : 32 * q + 4, :].bitcast(I32), tab2_scales[0, 4 * q : 4 * q + 4, :].bitcast(I32))
        load_w2(0)
        nc.sync.dma_start(w3_first[:], w3_view[:, 0 : 2 * P])
        nc.sync.dma_start(place[:], pos1)
        nc.sync.dma_start(wgs_t[:], wgs)
        for q in range(4):
            nc.sync.dma_start(w3_s[32 * q : 32 * q + 4, :].bitcast(I32), w3_scales[0, 4 * q : 4 * q + 4, :].bitcast(I32))
        load_w2(1)
        load_tab(0)
        nc.vector.tensor_copy(v2_s[:], tab2_s[:].indirect(idx2[:]))
        nc.vector.tensor_copy(v2_w[:], tab2_w[:].bitcast(U32).indirect(idx2[:]))
        nc.vector.tensor_copy(v_s0[:], tab_s[:].indirect(idx[:]))
        for plane in (v_s, w1_s):
            nc.vector.memset(plane[:].bitcast(I32), 0)
        nc.vector.memset(pages[0][:], 0.0)
        nc.vector.memset(gain_rows[:], 0.0)
        for a in range(2):
            for q in range(4):
                row = 96 + 16 * a + 4 * q
                nc.gpsimd.dma_start(v_s[32 * q : 32 * q + 4, a, :].bitcast(I32), v_s0[row : row + 4, :].bitcast(I32))
        load_tab(1)
        nc.sync.dma_start(w1_w[:].bitcast(I32), w1_words.rearrange("a p n -> p a n").bitcast(I32))
        for q in range(4):
            nc.sync.dma_start(
                w1_s[32 * q : 32 * q + 4, :, :].bitcast(I32),
                w1_scales[:, 4 * q : 4 * q + 4, :].rearrange("a r n -> r a n").bitcast(I32),
            )
        nc.sync.dma_start(gain_rows[0:ROW_TILES, :], gain.rearrange("(c p) -> c p", p=P))
        load_w2(2)
        nc.sync.dma_start(w3_rest[:], w3_view[:, 2 * P : H])
        load_base(0)
        load_w2(3)
        load_base(1)
        load_w2(4)
        load_base(2)
        load_w4(0)
        load_base(3)
        load_w4(1)
        load_base(4)
        load_base(5)
        load_base(6)
        load_base(7)

        v_w = [held("v_w%d" % a, [P, S], U32) for a in range(2)]

        def gather_tab(a):
            window = tab_w[a][:].bitcast(U32)
            if a == 0:
                nc.vector.tensor_copy(v_w[0][:], window.indirect(idx[:]))
            else:
                for h in range(2):
                    nc.vector.tensor_copy(v_w[1][:, BANK * h : BANK * (h + 1)], window.indirect(idx[:, 32 * h : 32 * (h + 1)]))

        gain_col = held("gain_col", [P, ROW_TILES], F32)

        def quantised(name, raw, width):
            grouped = ring.tile([P, width, 4], BF16, name="grouped", tag="grouped", align_bytes=64)
            nc.scalar.copy(
                grouped[:].rearrange("p (c i) t -> p c t i", i=4),
                raw[:].rearrange("p t (c i) -> p c t i", i=4),
            )
            codes = held(name + "_c", [P, width], U32)
            scales = held(name + "_s", [P, width], U8)
            nc.vector.quantize_mx(out=codes[:].bitcast(FP8X4), scales=scales[:], in_=grouped[:].rearrange("p w t -> p (w t)"))
            return codes, scales

        w2_q = {}
        w4_q = {}
        feat = {}
        both = {}
        z_t = {}
        z_q = {}
        acc = {}

        def assay(c):
            piece = max(i for i in range(5) if w2_cut[i] <= P * c)
            codes, scales = w2_q[piece]
            own = slice(P * c - w2_cut[piece], P * (c + 1) - w2_cut[piece])
            cols = slice(P * c, P * (c + 1))
            w3_cols = w3_first[:, P * c : P * (c + 1)] if c < 2 else w3_rest[:, P * (c - 2) : P * (c - 1)]
            y2 = bank("y2", [P, BANK])
            y3 = bank(("y3", "back1")[c % 2], [P, BANK])
            nc.tensor.matmul_mx(out=y2[:], lhsT=codes[:, own].bitcast(FP8X4), lhsT_scale=scales[:, own],
                                rhs=v2_w[:].bitcast(FP8X4), rhs_scale=v2_s[:], start=True, stop=True)
            nc.tensor.matmul_mx(out=y3[:], lhsT=w3_cols.bitcast(FP8X4), lhsT_scale=w3_s[:, cols],
                                rhs=v2_w[:].bitcast(FP8X4), rhs_scale=v2_s[:], start=True, stop=True)
            sq = ring.tile([P, NP], F32, name="sq")
            nc.scalar.activation(sq[:], y2[:], ACT.Square)
            both[c] = ring.tile([P, NP], F32, name="both")
            nc.vector.tensor_tensor(both[c][:], y3[:], sq[:], ALU.add)

        def put(c):
            nc.vector.tensor_tensor(pages[min(c, PAGES - 1)][:].indirect(place[:]), both[c][:], wgs_t[:], ALU.mult)

        def sensor(c):
            feat[c] = ring.tile([P, S], F32, name="feat", bufs=3)
            for h in range(2):
                x = bank("x%d" % h, [P, BANK])
                for a in range(2):
                    nc.tensor.matmul_mx(
                        out=x[:], lhsT=w1_w[:, a, 2 * P * c : 2 * P * (c + 1)].bitcast(FP4X4),
                        lhsT_scale=w1_s[:, a, P * c : P * (c + 1)],
                        rhs=v_w[a][:, BANK * h : BANK * (h + 1)].bitcast(FP8X4), rhs_scale=v_s[:, a, BANK * h : BANK * (h + 1)],
                        start=(a == 0), stop=(a == 1),
                    )
                nc.scalar.activation(feat[c][:, BANK * h : BANK * (h + 1)], x[:], ACT.Gelu_apprx_tanh)

        def combine(c, halves):
            b, cc = divmod(c, 4)
            f = feat[c]
            for cols in halves:
                nc.vector.tensor_tensor(f[:, cols], f[:, cols], pages[min(c, PAGES - 1)][:, cols], ALU.max)
                if (c, cols.start) in GAIN_ON_VECTOR:
                    nc.vector.tensor_scalar(f[:, cols], f[:, cols], gain_col[:, c : c + 1], None, ALU.mult)
                else:
                    nc.scalar.activation(f[:, cols], f[:, cols], ACT.Copy, scale=gain_col[:, c : c + 1])
            for h in range(2):
                if cc == 0:
                    z_t[b, h] = held("z_t%d%d" % (b, h), [P, 4, 2, P, 2], BF16)
                turned = bank("turn%d" % h, [P, 4, P])
                for step, src in enumerate((base_t[c], f)):
                    for k in range(4):
                        j0 = BANK * h + P * k
                        nc.tensor.matmul(turned[:, k, :], src[:, j0 : j0 + P], ident[:], is_transpose=True,
                                         start=(step == 0 and k == 0), stop=(step == 1 and k == 3))
                copy = nc.vector.tensor_copy if ("t", c, h) in TAIL_ON_VECTOR else nc.scalar.copy
                copy(
                    z_t[b, h][:, :, :, 32 * cc : 32 * (cc + 1), :],
                    turned[:].rearrange("j k (p u e) -> j k u p e", u=2, e=2),
                )

        def turn_back(b, h):
            words = z_t[b, h][:].rearrange("j k u p e -> j (k u p e)").bitcast(F32)
            grouped = ring.tile([P, BANK * 4], BF16, name="z_grouped", align_bytes=64)
            pairs = grouped[:].bitcast(F32).rearrange("p (j u) -> p j u", u=2)
            for quarter in range(2):
                back = bank("back%d" % (quarter * b), [P, 2, 2 * P])
                for k in range(2):
                    for u in range(2):
                        w0 = P * (2 * (2 * quarter + k) + u)
                        nc.tensor.transpose(back[:, u, P * k : P * (k + 1)], words[:, w0 : w0 + P], ident[:])
                copy = nc.vector.tensor_copy if ("b", b, h, quarter) in TAIL_ON_VECTOR else nc.scalar.copy
                copy(pairs[:, 256 * quarter : 256 * (quarter + 1), :], back[:].rearrange("p u j -> p j u"))
            codes = held("z_c%d%d" % (b, h), [P, BANK], U32)
            scales = held("z_s%d%d" % (b, h), [P, BANK], U8)
            nc.vector.quantize_mx(out=codes[:].bitcast(FP8X4), scales=scales[:], in_=grouped[:])
            z_q[b, h] = (codes, scales)

        out_banks = (("y2", "y3", "x0", "x1"), ("turn0", "turn1", "back0", "back1"))

        def last_product(b, h, tiles):
            wc, ws = w4_q[b]
            zc, zs = z_q[b, h]
            for n in tiles:
                if b == 0:
                    acc[n, h] = bank(out_banks[h][n], [P, BANK])
                cols = slice(P * n, P * (n + 1))
                nc.tensor.matmul_mx(out=acc[n, h][:], lhsT=wc[:, cols].bitcast(FP8X4), lhsT_scale=ws[:, cols],
                                    rhs=zc[:].bitcast(FP8X4), rhs_scale=zs[:], start=(b == 0), stop=(b == 1))
                if b == 1:
                    res = ring.tile([P, BANK], F32, name="res", bufs=8)
                    nc.scalar.activation(res[:], acc[n, h][:], ACT.Tanh)
                    nc.sync.dma_start(out[cols, BANK * h : BANK * (h + 1)], res[:])

        whole = [slice(0, S)]
        by_half = [slice(0, BANK), slice(BANK, S)]

        def w2_piece(i):
            w2_q[i] = quantised("w2q%d" % i, w2_raw[i], w2_cut[i + 1] - w2_cut[i])

        w2_piece(0)
        assay(0)
        put(0)
        w2_piece(1)
        assay(1)
        gather_tab(0)
        gather_tab(1)
        gain_ps = bank("back0", [P, P])
        nc.tensor.transpose(gain_ps[:], gain_rows[:], ident[:])
        nc.scalar.copy(gain_col[:], gain_ps[:, 0:ROW_TILES])
        sensor(0)
        pass
        w2_piece(2)
        for c in range(ROW_TILES):
            if c in (0, 1):
                w2_piece(3 + (0, 1).index(c))
            if c + 2 < ROW_TILES:
                assay(c + 2)
            if c + 1 < ROW_TILES:
                sensor(c + 1)
            combine(c, by_half if c == ROW_TILES - 1 else whole)
            if 0 < c + 1 < ROW_TILES:
                put(c + 1)
            if c == 1:
                w4_q[0] = quantised("w4q0", w4_raw[0], N)
            if c == 2:
                w4_q[1] = quantised("w4q1", w4_raw[1], N)
            if c == 3:
                turn_back(0, 0)
            if c == 3+0:
                turn_back(0, 1)
            if c == 6:
                last_product(0, 0, range(4))
        turn_back(1, 0)
        last_product(0, 1, range(2))
        last_product(1, 0, range(4))
        turn_back(1, 1)
        last_product(1, 1, range(2))
        for n in (2, 3):
            last_product(0, 1, [n])
            last_product(1, 1, [n])
